import numpy as np
import ml_dtypes


def mxq(x, axis, fmt="e4m3"):
    dtype, down = {"e4m3": (ml_dtypes.float8_e4m3fn, 7), "e5m2": (ml_dtypes.float8_e5m2, 14)}[fmt]
    v = np.moveaxis(np.asarray(x, np.float32).astype(ml_dtypes.bfloat16).astype(np.float64), axis, -1)
    blocks = v.reshape(v.shape[:-1] + (-1, 32))
    amax = np.abs(blocks).max(-1, keepdims=True)
    byte = np.maximum(np.where(amax > 0, np.frexp(amax)[1] - 1 + 127, 0) - down, 1)
    scale = np.exp2(byte - 127.0)
    codes = (blocks / scale).astype(np.float32).astype(dtype).astype(np.float64)
    return np.moveaxis((codes * scale).reshape(v.shape), -1, axis)


WIDE = False


def mx_kscale(k):
    if not WIDE:
        return np.ones(k)
    levels = np.array([10, -10, 5, -5, 0])
    if k % 512:
        return np.exp2(np.random.permutation(np.resize(levels, k // 32))).repeat(32)
    a = np.empty((k // 512, 16))
    for p in range(k // 512):
        a[p, :8] = np.random.permutation(np.resize(levels, 8))
        for g in range(8):
            far = levels[np.abs(levels - a[p, g]) >= 10]
            a[p, g + 8] = far[np.random.randint(len(far))]
    return np.exp2(a.ravel()).repeat(32)


def f64(x):
    return np.asarray(x).astype(np.float64)


def striped(idx):
    return np.tile(idx.reshape(-1, 16).T, (8, 1)).astype(np.uint16)


def unstriped(offs):
    return offs[:16].T.reshape(-1).astype(np.int64)

def planes(y):
    n, m = y.shape
    v = y.astype(np.float32).astype(ml_dtypes.bfloat16).astype(np.float64).reshape(n // 32, 32, m)
    top = np.abs(v).max(1)
    byte = np.clip(np.where(top > 0, np.frexp(top)[1] - 1 + 127 - 7, 1), 1, 254)
    codes = (v * np.exp2(127.0 - byte)[:, None, :]).reshape(n, m).astype(np.float32).astype(ml_dtypes.float8_e4m3fn).view(np.uint8)
    words = codes.reshape(n // 512, 128, 4, m).transpose(0, 1, 3, 2)
    return np.ascontiguousarray(words), np.ascontiguousarray(byte.astype(np.uint8).reshape(n // 512, 16, m))


K, T, S, H = 512, 1024, 512, 512


def setup_inputs():
    n = np.random.standard_normal
    s = mx_kscale(K)[:, None]
    u = mx_kscale(H)
    return {
        "xT": (n((K, T)) * s).astype(np.float32),
        "w1": (n((K, H)) / np.sqrt(K) / s * u).astype(np.float32),
        "w2": (n((H, H)) / np.sqrt(H) / u[:, None]).astype(np.float32),
        "pe": (0.5 * n((H, T)) * u[:, None]).astype(np.float32),
        "offs": striped(np.random.permutation(T)[:S]),
    }


def reference(xT, w1, w2, pe, offs):
    xq = mxq(f64(xT)[:, unstriped(offs)], 0, "e4m3")
    g = f64(pe)[:, unstriped(offs)]
    h = (mxq(f64(w1), 0, "e4m3").T @ xq) + g
    out_0 = mxq(f64(w2), 0, "e4m3").T @ mxq(h, 0, "e4m3")
    return (out_0,) + planes(out_0)

@@ -1,0 +1,181 @@
+from contextlib import ExitStack
+
+import concourse.mybir as mybir
+
+K, T, S, H = 512, 1024, 512, 512
+FLOPS = 2 * K * H * S + 2 * H * H * S
+
+F32 = mybir.dt.float32
+BF16 = mybir.dt.bfloat16
+I32 = mybir.dt.int32
+U32 = mybir.dt.uint32
+U16 = mybir.dt.uint16
+U8 = mybir.dt.uint8
+FP8X4 = mybir.dt.float8_e4m3fn_x4
+ADD = mybir.AluOpType.add
+
+P = 128
+PACK = 4
+RUN = 4
+QUARTER = 128
+QUARTERS = S // QUARTER
+W1_SPLIT = 64
+W_HALF = 256
+
+
+def interleave_views(dst, src):
+    return (
+        dst.rearrange("p (c i t) -> p c t i", i=RUN, t=PACK),
+        src.rearrange("p t (c i) -> p c t i", i=RUN),
+    )
+
+
+def quantize(nc, codes, scales, grouped):
+    nc.vector.quantize_mx(out=codes.bitcast(FP8X4), scales=scales, in_=grouped)
+
+
+def tile_picked_posadd_none_lo_kernel(tc, xT, w1, w2, pe, offs, out_0, out_1, out_2):
+    nc = tc.nc
+    with ExitStack() as ctx:
+        keep = ctx.enter_context(tc.tile_pool(name="keep", bufs=1))
+        psum = ctx.enter_context(tc.psum_pool(name="psum", bufs=1))
+
+        offsets = keep.tile([P, S // 16], U16, name="offsets")
+        nc.sync.dma_start(offsets[:], offs)
+
+        x_rows = xT.rearrange("(p t) c -> p t c", t=PACK)
+        pe_rows = pe.rearrange("(p t) c -> p t c", t=PACK)
+        w1_rows = w1.rearrange("(p j) c -> p j c", j=PACK)
+        w2_rows = w2.rearrange("(p j) c -> p j c", j=PACK)
+
+        x_table = [keep.tile([P, T], F32, name="x_table%d" % t) for t in range(PACK)]
+        pe_table = [keep.tile([P, T], F32, name="pe_table%d" % t) for t in range(PACK)]
+        w1_raw = keep.tile([P, PACK, H], F32, name="w1_raw")
+        w2_raw = [keep.tile([P, PACK, W_HALF], F32, name="w2_raw%d" % a) for a in range(2)]
+
+        for t in range(PACK):
+            nc.sync.dma_start(x_table[t][:], x_rows[:, t, :])
+        for t in range(PACK - 1):
+            nc.sync.dma_start(pe_table[t][:], pe_rows[:, t, :])
+        nc.sync.dma_start(w1_raw[:], w1_rows)
+        nc.sync.dma_start(pe_table[PACK - 1][:], pe_rows[:, PACK - 1, :])
+        for a in range(2):
+            nc.sync.dma_start(w2_raw[a][:], w2_rows[:, :, a * W_HALF : (a + 1) * W_HALF])
+
+        x_picked = keep.tile([P, PACK, S], F32, name="x_picked")
+        pe_and_w1 = keep.tile([P, (PACK + 1) * S], F32, name="pe_and_w1", align_bytes=64)
+        pe_picked = pe_and_w1[:, : PACK * S].rearrange("p (t n) -> p t n", t=PACK)
+        w1_grouped = pe_and_w1[:, (PACK - 1) * S :].bitcast(BF16)
+        x_grouped = keep.tile([P, S * PACK], BF16, name="x_grouped", align_bytes=64)
+        x_codes = keep.tile([P, S], U32, name="x_codes", align_bytes=64)
+        x_scales = keep.tile([P, S], U8, name="x_scales", align_bytes=64)
+        w1_codes = keep.tile([P, H], U32, name="w1_codes", align_bytes=64)
+        w1_scales = keep.tile([P, H], U8, name="w1_scales", align_bytes=64)
+        w2_grouped = keep.tile([P, PACK * H], BF16, name="w2_grouped", align_bytes=64)
+        w2_codes = keep.tile([P, H], U32, name="w2_codes", align_bytes=64)
+        w2_scales = keep.tile([P, H], U8, name="w2_scales", align_bytes=64)
+        h_first = keep.tile([P, 2 * QUARTER * PACK], BF16, name="h_first", align_bytes=64)
+        h_codes = keep.tile([P, S], U32, name="h_codes", align_bytes=64)
+        h_scales = keep.tile([P, S], U8, name="h_scales", align_bytes=64)
+        y = keep.tile([P, PACK, S], F32, name="y")
+        y_grouped = keep.tile([P, S * PACK], BF16, name="y_grouped", align_bytes=64)
+        y_codes = keep.tile([P, S], U32, name="y_codes", align_bytes=64)
+        y_scales = keep.tile([P, S], U8, name="y_scales", align_bytes=64)
+        h_bank = [psum.tile([P, PACK, QUARTER], F32, name="h_bank%d" % q) for q in range(QUARTERS)]
+        y_bank = [psum.tile([P, PACK, QUARTER], F32, name="y_bank%d" % q) for q in range(QUARTERS)]
+        wide = QUARTER * PACK
+        h_grouped = [h_first[:, :wide], h_first[:, wide:], w2_grouped[:, :wide], w2_grouped[:, wide : 2 * wide]]
+
+        def deal(copy, grouped, raw, first, m0, m1):
+            dst = grouped.rearrange("p (t m j) -> p m j t", t=PACK, j=PACK)[:, m0:m1, :, :]
+            src = raw[:].rearrange("p j (m t) -> p m j t", t=PACK)[:, m0 - first : m1 - first, :, :]
+            copy(out=dst, in_=src)
+
+        def product(bank, w_codes, w_scales, codes, scales, cols):
+            for t in range(PACK):
+                w_cols = slice(t * P, (t + 1) * P)
+                nc.tensor.matmul_mx(
+                    out=bank[:, t, :],
+                    lhsT=w_codes[:, w_cols].bitcast(FP8X4),
+                    lhsT_scale=w_scales[:, w_cols],
+                    rhs=codes[:, cols].bitcast(FP8X4),
+                    rhs_scale=scales[:, cols],
+                    start=True,
+                    stop=True,
+                )
+
+        for t in range(PACK):
+            nc.vector.tensor_copy(x_picked[:, t, :], x_table[t][:].indirect(offsets[:]))
+        for a in range(2):
+            cols = slice(a * 256, (a + 1) * 256)
+            wcols = slice(a * 1024, (a + 1) * 1024)
+            dst, src = interleave_views(x_grouped[:, wcols], x_picked[:, :, cols])
+            nc.scalar.copy(out=dst, in_=src)
+            nc.vector.tensor_copy(pe_picked[:, a, :], pe_table[a][:].indirect(offsets[:]))
+            quantize(nc, x_codes[:, cols], x_scales[:, cols], x_grouped[:, wcols])
+        nc.vector.tensor_copy(pe_picked[:, 2, :], pe_table[2][:].indirect(offsets[:]))
+        deal(nc.scalar.copy, w1_grouped, w1_raw, 0, W1_SPLIT, P)
+        deal(nc.vector.tensor_copy, w1_grouped, w1_raw, 0, 0, W1_SPLIT)
+        quantize(nc, w1_codes[:], w1_scales[:], w1_grouped)
+        for q in range(QUARTERS):
+            product(h_bank[q], w1_codes, w1_scales, x_codes, x_scales, slice(q * QUARTER, (q + 1) * QUARTER))
+        nc.vector.tensor_copy(pe_picked[:, 3, :], pe_table[3][:].indirect(offsets[:]))
+
+        deal(nc.scalar.copy, w2_grouped[:], w2_raw[0], 0, 0, 64)
+        deal(nc.scalar.copy, w2_grouped[:], w2_raw[1], 64, 64, 128)
+
+        def add(q):
+            cols = slice(q * QUARTER, (q + 1) * QUARTER)
+            dst, src = interleave_views(h_grouped[q], pe_picked[:, :, cols])
+            acc = h_bank[q][:].rearrange("p t (c i) -> p c t i", i=RUN)
+            nc.vector.tensor_tensor(out=dst, in0=acc, in1=src, op=ADD)
+
+        def quantize_h(first, count, grouped):
+            cols = slice(first * QUARTER, (first + count) * QUARTER)
+            quantize(nc, h_codes[:, cols], h_scales[:, cols], grouped)
+
+        out_rows = out_0.rearrange("(p t) n -> p t n", t=PACK)
+        words = out_1.rearrange("z p n r -> p (z n r)").bitcast(I32)
+
+        def second(q):
+            cols = slice(q * QUARTER, (q + 1) * QUARTER)
+            product(y_bank[q], w2_codes, w2_scales, h_codes, h_scales, cols)
+            nc.scalar.copy(out=y[:, :, cols], in_=y_bank[q][:])
+            nc.sync.dma_start(out_rows[:, :, cols], y[:, :, cols])
+
+        def regroup(q, on_scalar):
+            cols = slice(q * QUARTER, (q + 1) * QUARTER)
+            wcols = slice(q * wide, (q + 1) * wide)
+            if on_scalar:
+                nc.scalar.copy(out=y_grouped[:, wcols].rearrange("p (n t) -> p n t", t=PACK), in_=y_bank[q][:].rearrange("p t n -> p n t"))
+            else:
+                dst, src = interleave_views(y_grouped[:, wcols], y[:, :, cols])
+                nc.vector.tensor_copy(out=dst, in_=src)
+
+        def quantize_y(first, count):
+            cols = slice(first * QUARTER, (first + count) * QUARTER)
+            quantize(nc, y_codes[:, cols], y_scales[:, cols], y_grouped[:, first * wide : (first + count) * wide])
+            nc.sync.dma_start(words[:, cols], y_codes[:, cols].bitcast(I32))
+
+        add(0)
+        add(1)
+        quantize(nc, w2_codes[:], w2_scales[:], w2_grouped[:])
+        quantize_h(0, 2, h_first[:])
+        add(2)
+        add(3)
+        quantize_h(2, 1, h_grouped[2])
+        quantize_h(3, 1, h_grouped[3])
+        second(0)
+        second(1)
+        regroup(0, False)
+        regroup(1, False)
+        second(2)
+        second(3)
+        quantize_y(0, 2)
+        regroup(2, False)
+        regroup(3, False)
+        quantize_y(2, 2)
+        scale_rows = out_2.rearrange("z q n -> (z q) n").bitcast(I32)
+        for g in range(4):
+            queue = nc.sync if g % 2 == 0 else nc.scalar
+            queue.dma_start(scale_rows[4 * g : 4 * g + 4, :], y_scales[32 * g : 32 * g + 4, :].bitcast(I32))

@@ -19,8 +19,9 @@ PACK = 4
 RUN = 4
 QUARTER = 128
 QUARTERS = S // QUARTER
-W1_SPLIT = 64
+W1_SPLIT = 40
 W_HALF = 256
+W2_SPLIT = 32
 
 
 def interleave_views(dst, src):
@@ -51,14 +52,15 @@ def tile_picked_posadd_none_lo_kernel(tc, xT, w1, w2, pe, offs, out_0, out_1, ou
         x_table = [keep.tile([P, T], F32, name="x_table%d" % t) for t in range(PACK)]
         pe_table = [keep.tile([P, T], F32, name="pe_table%d" % t) for t in range(PACK)]
         w1_raw = keep.tile([P, PACK, H], F32, name="w1_raw")
-        w2_raw = [keep.tile([P, PACK, W_HALF], F32, name="w2_raw%d" % a) for a in range(2)]
+        w2_raw = [keep.tile([P, PACK, W_HALF], F32, name="w2_raw%d" % a, tag="w2_raw%d" % a, align_bytes=64) for a in range(2)]
 
         for t in range(PACK):
             nc.sync.dma_start(x_table[t][:], x_rows[:, t, :])
-        for t in range(PACK - 1):
+        for t in range(2):
             nc.sync.dma_start(pe_table[t][:], pe_rows[:, t, :])
         nc.sync.dma_start(w1_raw[:], w1_rows)
-        nc.sync.dma_start(pe_table[PACK - 1][:], pe_rows[:, PACK - 1, :])
+        for t in range(2, PACK):
+            nc.sync.dma_start(pe_table[t][:], pe_rows[:, t, :])
         for a in range(2):
             nc.sync.dma_start(w2_raw[a][:], w2_rows[:, :, a * W_HALF : (a + 1) * W_HALF])
 
@@ -75,7 +77,6 @@ def tile_picked_posadd_none_lo_kernel(tc, xT, w1, w2, pe, offs, out_0, out_1, ou
         w2_codes = keep.tile([P, H], U32, name="w2_codes", align_bytes=64)
         w2_scales = keep.tile([P, H], U8, name="w2_scales", align_bytes=64)
         h_first = keep.tile([P, 2 * QUARTER * PACK], BF16, name="h_first", align_bytes=64)
-        h_codes = keep.tile([P, S], U32, name="h_codes", align_bytes=64)
         h_scales = keep.tile([P, S], U8, name="h_scales", align_bytes=64)
         y = keep.tile([P, PACK, S], F32, name="y")
         y_grouped = keep.tile([P, S * PACK], BF16, name="y_grouped", align_bytes=64)
@@ -91,11 +92,11 @@ def tile_picked_posadd_none_lo_kernel(tc, xT, w1, w2, pe, offs, out_0, out_1, ou
             src = raw[:].rearrange("p j (m t) -> p m j t", t=PACK)[:, m0 - first : m1 - first, :, :]
             copy(out=dst, in_=src)
 
-        def product(bank, w_codes, w_scales, codes, scales, cols):
-            for t in range(PACK):
+        def product(bank, w_codes, w_scales, codes, scales, cols, first=0, count=PACK):
+            for t in range(first, first + count):
                 w_cols = slice(t * P, (t + 1) * P)
                 nc.tensor.matmul_mx(
-                    out=bank[:, t, :],
+                    out=bank[:, t - first, :],
                     lhsT=w_codes[:, w_cols].bitcast(FP8X4),
                     lhsT_scale=w_scales[:, w_cols],
                     rhs=codes[:, cols].bitcast(FP8X4),
@@ -106,23 +107,21 @@ def tile_picked_posadd_none_lo_kernel(tc, xT, w1, w2, pe, offs, out_0, out_1, ou
 
         for t in range(PACK):
             nc.vector.tensor_copy(x_picked[:, t, :], x_table[t][:].indirect(offsets[:]))
-        for a in range(2):
-            cols = slice(a * 256, (a + 1) * 256)
-            wcols = slice(a * 1024, (a + 1) * 1024)
-            dst, src = interleave_views(x_grouped[:, wcols], x_picked[:, :, cols])
-            nc.scalar.copy(out=dst, in_=src)
-            nc.vector.tensor_copy(pe_picked[:, a, :], pe_table[a][:].indirect(offsets[:]))
-            quantize(nc, x_codes[:, cols], x_scales[:, cols], x_grouped[:, wcols])
-        nc.vector.tensor_copy(pe_picked[:, 2, :], pe_table[2][:].indirect(offsets[:]))
+        dst, src = interleave_views(x_grouped[:], x_picked[:])
+        nc.scalar.copy(out=dst, in_=src)
+        for t in range(2):
+            nc.vector.tensor_copy(pe_picked[:, t, :], pe_table[t][:].indirect(offsets[:]))
+        quantize(nc, x_codes[:], x_scales[:], x_grouped[:])
         deal(nc.scalar.copy, w1_grouped, w1_raw, 0, W1_SPLIT, P)
         deal(nc.vector.tensor_copy, w1_grouped, w1_raw, 0, 0, W1_SPLIT)
+        nc.vector.tensor_copy(pe_picked[:, 2, :], pe_table[2][:].indirect(offsets[:]))
         quantize(nc, w1_codes[:], w1_scales[:], w1_grouped)
         for q in range(QUARTERS):
             product(h_bank[q], w1_codes, w1_scales, x_codes, x_scales, slice(q * QUARTER, (q + 1) * QUARTER))
         nc.vector.tensor_copy(pe_picked[:, 3, :], pe_table[3][:].indirect(offsets[:]))
 
         deal(nc.scalar.copy, w2_grouped[:], w2_raw[0], 0, 0, 64)
-        deal(nc.scalar.copy, w2_grouped[:], w2_raw[1], 64, 64, 128)
+        deal(nc.scalar.copy, w2_grouped[:], w2_raw[1], 64, 64 + W2_SPLIT, 128)
 
         def add(q):
             cols = slice(q * QUARTER, (q + 1) * QUARTER)
@@ -143,6 +142,21 @@ def tile_picked_posadd_none_lo_kernel(tc, xT, w1, w2, pe, offs, out_0, out_1, ou
             nc.scalar.copy(out=y[:, :, cols], in_=y_bank[q][:])
             nc.sync.dma_start(out_rows[:, :, cols], y[:, :, cols])
 
+        def second_part(bank, cols, first, count):
+            product(bank, w2_codes, w2_scales, h_codes, h_scales, cols, first, count)
+            nc.scalar.copy(out=y[:, first : first + count, cols], in_=bank)
+
+        def store(cols, first, count):
+            nc.sync.dma_start(out_rows[:, first : first + count, cols], y[:, first : first + count, cols])
+
+        def regroup_wide(first, count):
+            cols = slice(first * QUARTER, (first + count) * QUARTER)
+            dst, src = interleave_views(y_grouped[:, first * wide : (first + count) * wide], y[:, :, cols])
+            nc.vector.tensor_copy(out=dst, in_=src)
+
+        def as_half(bank):
+            return bank[:].rearrange("p t n -> p (t n)").rearrange("p (t n) -> p t n", t=2)
+
         def regroup(q, on_scalar):
             cols = slice(q * QUARTER, (q + 1) * QUARTER)
             wcols = slice(q * wide, (q + 1) * wide)
@@ -159,19 +173,24 @@ def tile_picked_posadd_none_lo_kernel(tc, xT, w1, w2, pe, offs, out_0, out_1, ou
 
         add(0)
         add(1)
-        quantize(nc, w2_codes[:], w2_scales[:], w2_grouped[:])
+        deal(nc.vector.tensor_copy, w2_grouped[:], w2_raw[1], 64, 64, 64 + W2_SPLIT)
+        h_codes = keep.tile([P, S], U32, name="h_codes", tag="w2_raw1", align_bytes=64)
         quantize_h(0, 2, h_first[:])
+        quantize(nc, w2_codes[:], w2_scales[:], w2_grouped[:])
         add(2)
         add(3)
         quantize_h(2, 1, h_grouped[2])
         quantize_h(3, 1, h_grouped[3])
-        second(0)
-        second(1)
-        regroup(0, False)
-        regroup(1, False)
+        second_part(as_half(y_bank[0]), slice(0, 256), 0, 2)
+        store(slice(0, 256), 0, 2)
+        second_part(as_half(y_bank[1]), slice(0, 256), 2, 2)
+        store(slice(0, 256), 2, 2)
+        regroup_wide(0, 2)
         second(2)
-        second(3)
         quantize_y(0, 2)
+        second_part(y_bank[3][:, 0:2, :], slice(384, 512), 0, 2)
+        second_part(h_bank[0][:, 0:2, :], slice(384, 512), 2, 2)
+        store(slice(384, 512), 0, 4)
         regroup(2, False)
         regroup(3, False)
         quantize_y(2, 2)

@@ -21,7 +21,7 @@ QUARTER = 128
 QUARTERS = S // QUARTER
 W1_SPLIT = 40
 W_HALF = 256
-W2_SPLIT = 32
+W2_SPLIT = 0
 
 
 def interleave_views(dst, src):
@@ -82,7 +82,9 @@ def tile_picked_posadd_none_lo_kernel(tc, xT, w1, w2, pe, offs, out_0, out_1, ou
         y_grouped = keep.tile([P, S * PACK], BF16, name="y_grouped", align_bytes=64)
         y_codes = keep.tile([P, S], U32, name="y_codes", align_bytes=64)
         y_scales = keep.tile([P, S], U8, name="y_scales", align_bytes=64)
-        h_bank = [psum.tile([P, PACK, QUARTER], F32, name="h_bank%d" % q) for q in range(QUARTERS)]
+        h_pair = [psum.tile([P, PACK, QUARTER], F32, name="h_bank%d" % q) for q in range(2)]
+        h_bank = h_pair + h_pair
+        y_last = psum.tile([P, 2, QUARTER], F32, name="y_last")
         y_bank = [psum.tile([P, PACK, QUARTER], F32, name="y_bank%d" % q) for q in range(QUARTERS)]
         wide = QUARTER * PACK
         h_grouped = [h_first[:, :wide], h_first[:, wide:], w2_grouped[:, :wide], w2_grouped[:, wide : 2 * wide]]
@@ -92,11 +94,11 @@ def tile_picked_posadd_none_lo_kernel(tc, xT, w1, w2, pe, offs, out_0, out_1, ou
             src = raw[:].rearrange("p j (m t) -> p m j t", t=PACK)[:, m0 - first : m1 - first, :, :]
             copy(out=dst, in_=src)
 
-        def product(bank, w_codes, w_scales, codes, scales, cols, first=0, count=PACK):
-            for t in range(first, first + count):
+        def product(bank, w_codes, w_scales, codes, scales, cols, start=0, count=PACK):
+            for t in range(start, start + count):
                 w_cols = slice(t * P, (t + 1) * P)
                 nc.tensor.matmul_mx(
-                    out=bank[:, t - first, :],
+                    out=bank[:, t - start, :],
                     lhsT=w_codes[:, w_cols].bitcast(FP8X4),
                     lhsT_scale=w_scales[:, w_cols],
                     rhs=codes[:, cols].bitcast(FP8X4),
@@ -116,8 +118,11 @@ def tile_picked_posadd_none_lo_kernel(tc, xT, w1, w2, pe, offs, out_0, out_1, ou
         deal(nc.vector.tensor_copy, w1_grouped, w1_raw, 0, 0, W1_SPLIT)
         nc.vector.tensor_copy(pe_picked[:, 2, :], pe_table[2][:].indirect(offsets[:]))
         quantize(nc, w1_codes[:], w1_scales[:], w1_grouped)
-        for q in range(QUARTERS):
+        def first(q):
             product(h_bank[q], w1_codes, w1_scales, x_codes, x_scales, slice(q * QUARTER, (q + 1) * QUARTER))
+
+        first(0)
+        first(1)
         nc.vector.tensor_copy(pe_picked[:, 3, :], pe_table[3][:].indirect(offsets[:]))
 
         deal(nc.scalar.copy, w2_grouped[:], w2_raw[0], 0, 0, 64)
@@ -171,11 +176,13 @@ def tile_picked_posadd_none_lo_kernel(tc, xT, w1, w2, pe, offs, out_0, out_1, ou
             quantize(nc, y_codes[:, cols], y_scales[:, cols], y_grouped[:, first * wide : (first + count) * wide])
             nc.sync.dma_start(words[:, cols], y_codes[:, cols].bitcast(I32))
 
+        h_codes = keep.tile([P, S], U32, name="h_codes", align_bytes=64)
         add(0)
+        first(2)
         add(1)
-        deal(nc.vector.tensor_copy, w2_grouped[:], w2_raw[1], 64, 64, 64 + W2_SPLIT)
-        h_codes = keep.tile([P, S], U32, name="h_codes", tag="w2_raw1", align_bytes=64)
-        quantize_h(0, 2, h_first[:])
+        first(3)
+        quantize_h(0, 1, h_grouped[0])
+        quantize_h(1, 1, h_grouped[1])
         quantize(nc, w2_codes[:], w2_scales[:], w2_grouped[:])
         add(2)
         add(3)
@@ -189,7 +196,7 @@ def tile_picked_posadd_none_lo_kernel(tc, xT, w1, w2, pe, offs, out_0, out_1, ou
         second(2)
         quantize_y(0, 2)
         second_part(y_bank[3][:, 0:2, :], slice(384, 512), 0, 2)
-        second_part(h_bank[0][:, 0:2, :], slice(384, 512), 2, 2)
+        second_part(y_last[:], slice(384, 512), 2, 2)
         store(slice(384, 512), 0, 4)
         regroup(2, False)
         regroup(3, False)

from contextlib import ExitStack

import concourse.mybir as mybir

K, T, S, H = 512, 1024, 512, 512
FLOPS = 2 * K * H * S + 2 * H * H * S

F32 = mybir.dt.float32
BF16 = mybir.dt.bfloat16
I32 = mybir.dt.int32
U32 = mybir.dt.uint32
U16 = mybir.dt.uint16
U8 = mybir.dt.uint8
FP8X4 = mybir.dt.float8_e4m3fn_x4
ADD = mybir.AluOpType.add

P = 128
PACK = 4
RUN = 4
QUARTER = 128
QUARTERS = S // QUARTER
W1_SPLIT = 40
W_HALF = 256
W2_SPLIT = 0


def interleave_views(dst, src):
    return (
        dst.rearrange("p (c i t) -> p c t i", i=RUN, t=PACK),
        src.rearrange("p t (c i) -> p c t i", i=RUN),
    )


def quantize(nc, codes, scales, grouped):
    nc.vector.quantize_mx(out=codes.bitcast(FP8X4), scales=scales, in_=grouped)


def tile_picked_posadd_none_lo_kernel(tc, xT, w1, w2, pe, offs, out_0, out_1, out_2):
    nc = tc.nc
    with ExitStack() as ctx:
        keep = ctx.enter_context(tc.tile_pool(name="keep", bufs=1))
        psum = ctx.enter_context(tc.psum_pool(name="psum", bufs=1))

        offsets = keep.tile([P, S // 16], U16, name="offsets")
        nc.sync.dma_start(offsets[:], offs)

        x_rows = xT.rearrange("(p t) c -> p t c", t=PACK)
        pe_rows = pe.rearrange("(p t) c -> p t c", t=PACK)
        w1_rows = w1.rearrange("(p j) c -> p j c", j=PACK)
        w2_rows = w2.rearrange("(p j) c -> p j c", j=PACK)

        x_table = [keep.tile([P, T], F32, name="x_table%d" % t) for t in range(PACK)]
        pe_table = [keep.tile([P, T], F32, name="pe_table%d" % t) for t in range(PACK)]
        w1_raw = keep.tile([P, PACK, H], F32, name="w1_raw")
        w2_raw = [keep.tile([P, PACK, W_HALF], F32, name="w2_raw%d" % a, tag="w2_raw%d" % a, align_bytes=64) for a in range(2)]

        for t in range(PACK):
            nc.sync.dma_start(x_table[t][:], x_rows[:, t, :])
        for t in range(2):
            nc.sync.dma_start(pe_table[t][:], pe_rows[:, t, :])
        nc.sync.dma_start(w1_raw[:], w1_rows)
        for t in range(2, PACK):
            nc.sync.dma_start(pe_table[t][:], pe_rows[:, t, :])
        for a in range(2):
            nc.sync.dma_start(w2_raw[a][:], w2_rows[:, :, a * W_HALF : (a + 1) * W_HALF])

        x_picked = keep.tile([P, PACK, S], F32, name="x_picked")
        pe_and_w1 = keep.tile([P, (PACK + 1) * S], F32, name="pe_and_w1", align_bytes=64)
        pe_picked = pe_and_w1[:, : PACK * S].rearrange("p (t n) -> p t n", t=PACK)
        w1_grouped = pe_and_w1[:, (PACK - 1) * S :].bitcast(BF16)
        x_grouped = keep.tile([P, S * PACK], BF16, name="x_grouped", align_bytes=64)
        x_codes = keep.tile([P, S], U32, name="x_codes", align_bytes=64)
        x_scales = keep.tile([P, S], U8, name="x_scales", align_bytes=64)
        w1_codes = keep.tile([P, H], U32, name="w1_codes", align_bytes=64)
        w1_scales = keep.tile([P, H], U8, name="w1_scales", align_bytes=64)
        w2_grouped = keep.tile([P, PACK * H], BF16, name="w2_grouped", align_bytes=64)
        w2_codes = keep.tile([P, H], U32, name="w2_codes", align_bytes=64)
        w2_scales = keep.tile([P, H], U8, name="w2_scales", align_bytes=64)
        h_first = keep.tile([P, 2 * QUARTER * PACK], BF16, name="h_first", align_bytes=64)
        h_scales = keep.tile([P, S], U8, name="h_scales", align_bytes=64)
        y = keep.tile([P, PACK, S], F32, name="y")
        y_grouped = keep.tile([P, S * PACK], BF16, name="y_grouped", align_bytes=64)
        y_codes = keep.tile([P, S], U32, name="y_codes", align_bytes=64)
        y_scales = keep.tile([P, S], U8, name="y_scales", align_bytes=64)
        h_pair = [psum.tile([P, PACK, QUARTER], F32, name="h_bank%d" % q) for q in range(2)]
        h_bank = h_pair + h_pair
        y_last = psum.tile([P, 2, QUARTER], F32, name="y_last")
        y_bank = [psum.tile([P, PACK, QUARTER], F32, name="y_bank%d" % q) for q in range(QUARTERS)]
        wide = QUARTER * PACK
        h_grouped = [h_first[:, :wide], h_first[:, wide:], w2_grouped[:, :wide], w2_grouped[:, wide : 2 * wide]]

        def deal(copy, grouped, raw, first, m0, m1):
            dst = grouped.rearrange("p (t m j) -> p m j t", t=PACK, j=PACK)[:, m0:m1, :, :]
            src = raw[:].rearrange("p j (m t) -> p m j t", t=PACK)[:, m0 - first : m1 - first, :, :]
            copy(out=dst, in_=src)

        def product(bank, w_codes, w_scales, codes, scales, cols, start=0, count=PACK):
            for t in range(start, start + count):
                w_cols = slice(t * P, (t + 1) * P)
                nc.tensor.matmul_mx(
                    out=bank[:, t - start, :],
                    lhsT=w_codes[:, w_cols].bitcast(FP8X4),
                    lhsT_scale=w_scales[:, w_cols],
                    rhs=codes[:, cols].bitcast(FP8X4),
                    rhs_scale=scales[:, cols],
                    start=True,
                    stop=True,
                )

        for t in range(PACK):
            nc.vector.tensor_copy(x_picked[:, t, :], x_table[t][:].indirect(offsets[:]))
        dst, src = interleave_views(x_grouped[:], x_picked[:])
        nc.scalar.copy(out=dst, in_=src)
        for t in range(2):
            nc.vector.tensor_copy(pe_picked[:, t, :], pe_table[t][:].indirect(offsets[:]))
        quantize(nc, x_codes[:], x_scales[:], x_grouped[:])
        deal(nc.scalar.copy, w1_grouped, w1_raw, 0, W1_SPLIT, P)
        deal(nc.vector.tensor_copy, w1_grouped, w1_raw, 0, 0, W1_SPLIT)
        nc.vector.tensor_copy(pe_picked[:, 2, :], pe_table[2][:].indirect(offsets[:]))
        quantize(nc, w1_codes[:], w1_scales[:], w1_grouped)
        def first(q):
            product(h_bank[q], w1_codes, w1_scales, x_codes, x_scales, slice(q * QUARTER, (q + 1) * QUARTER))

        first(0)
        first(1)
        nc.vector.tensor_copy(pe_picked[:, 3, :], pe_table[3][:].indirect(offsets[:]))

        deal(nc.scalar.copy, w2_grouped[:], w2_raw[0], 0, 0, 64)
        deal(nc.scalar.copy, w2_grouped[:], w2_raw[1], 64, 64 + W2_SPLIT, 128)

        def add(q):
            cols = slice(q * QUARTER, (q + 1) * QUARTER)
            dst, src = interleave_views(h_grouped[q], pe_picked[:, :, cols])
            acc = h_bank[q][:].rearrange("p t (c i) -> p c t i", i=RUN)
            nc.vector.tensor_tensor(out=dst, in0=acc, in1=src, op=ADD)

        def quantize_h(first, count, grouped):
            cols = slice(first * QUARTER, (first + count) * QUARTER)
            quantize(nc, h_codes[:, cols], h_scales[:, cols], grouped)

        out_rows = out_0.rearrange("(p t) n -> p t n", t=PACK)
        words = out_1.rearrange("z p n r -> p (z n r)").bitcast(I32)

        def second(q):
            cols = slice(q * QUARTER, (q + 1) * QUARTER)
            product(y_bank[q], w2_codes, w2_scales, h_codes, h_scales, cols)
            nc.scalar.copy(out=y[:, :, cols], in_=y_bank[q][:])
            nc.sync.dma_start(out_rows[:, :, cols], y[:, :, cols])

        def second_part(bank, cols, first, count):
            product(bank, w2_codes, w2_scales, h_codes, h_scales, cols, first, count)
            nc.scalar.copy(out=y[:, first : first + count, cols], in_=bank)

        def store(cols, first, count):
            nc.sync.dma_start(out_rows[:, first : first + count, cols], y[:, first : first + count, cols])

        def regroup_wide(first, count):
            cols = slice(first * QUARTER, (first + count) * QUARTER)
            dst, src = interleave_views(y_grouped[:, first * wide : (first + count) * wide], y[:, :, cols])
            nc.vector.tensor_copy(out=dst, in_=src)

        def as_half(bank):
            return bank[:].rearrange("p t n -> p (t n)").rearrange("p (t n) -> p t n", t=2)

        def regroup(q, on_scalar):
            cols = slice(q * QUARTER, (q + 1) * QUARTER)
            wcols = slice(q * wide, (q + 1) * wide)
            if on_scalar:
                nc.scalar.copy(out=y_grouped[:, wcols].rearrange("p (n t) -> p n t", t=PACK), in_=y_bank[q][:].rearrange("p t n -> p n t"))
            else:
                dst, src = interleave_views(y_grouped[:, wcols], y[:, :, cols])
                nc.vector.tensor_copy(out=dst, in_=src)

        def quantize_y(first, count):
            cols = slice(first * QUARTER, (first + count) * QUARTER)
            quantize(nc, y_codes[:, cols], y_scales[:, cols], y_grouped[:, first * wide : (first + count) * wide])
            nc.sync.dma_start(words[:, cols], y_codes[:, cols].bitcast(I32))

        h_codes = keep.tile([P, S], U32, name="h_codes", align_bytes=64)
        add(0)
        first(2)
        add(1)
        first(3)
        quantize_h(0, 1, h_grouped[0])
        quantize_h(1, 1, h_grouped[1])
        quantize(nc, w2_codes[:], w2_scales[:], w2_grouped[:])
        add(2)
        add(3)
        quantize_h(2, 1, h_grouped[2])
        quantize_h(3, 1, h_grouped[3])
        second_part(as_half(y_bank[0]), slice(0, 256), 0, 2)
        store(slice(0, 256), 0, 2)
        second_part(as_half(y_bank[1]), slice(0, 256), 2, 2)
        store(slice(0, 256), 2, 2)
        regroup_wide(0, 2)
        second(2)
        quantize_y(0, 2)
        second_part(y_bank[3][:, 0:2, :], slice(384, 512), 0, 2)
        second_part(y_last[:], slice(384, 512), 2, 2)
        store(slice(384, 512), 0, 4)
        regroup(2, False)
        regroup(3, False)
        quantize_y(2, 2)
        scale_rows = out_2.rearrange("z q n -> (z q) n").bitcast(I32)
        for g in range(4):
            queue = nc.sync if g % 2 == 0 else nc.scalar
            queue.dma_start(scale_rows[4 * g : 4 * g + 4, :], y_scales[32 * g : 32 * g + 4, :].bitcast(I32))
